import numpy as np
import ml_dtypes


def mxq(x, axis, fmt="e4m3"):
    dtype, down = {"e4m3": (ml_dtypes.float8_e4m3fn, 7), "e5m2": (ml_dtypes.float8_e5m2, 14)}[fmt]
    v = np.moveaxis(np.asarray(x, np.float32).astype(ml_dtypes.bfloat16).astype(np.float64), axis, -1)
    blocks = v.reshape(v.shape[:-1] + (-1, 32))
    amax = np.abs(blocks).max(-1, keepdims=True)
    byte = np.maximum(np.where(amax > 0, np.frexp(amax)[1] - 1 + 127, 0) - down, 1)
    scale = np.exp2(byte - 127.0)
    codes = (blocks / scale).astype(np.float32).astype(dtype).astype(np.float64)
    return np.moveaxis((codes * scale).reshape(v.shape), -1, axis)


WIDE = False


def mx_kscale(k):
    if not WIDE:
        return np.ones(k)
    levels = np.array([10, -10, 5, -5, 0])
    if k % 512:
        return np.exp2(np.random.permutation(np.resize(levels, k // 32))).repeat(32)
    a = np.empty((k // 512, 16))
    for p in range(k // 512):
        a[p, :8] = np.random.permutation(np.resize(levels, 8))
        for g in range(8):
            far = levels[np.abs(levels - a[p, g]) >= 10]
            a[p, g + 8] = far[np.random.randint(len(far))]
    return np.exp2(a.ravel()).repeat(32)


def f64(x):
    return np.asarray(x).astype(np.float64)


def striped8(idx):
    return np.concatenate([v.reshape(-1, 16).T for v in idx]).astype(np.uint16)


def unstriped8(offs):
    return np.stack([offs[16 * g:16 * g + 16].T.reshape(-1) for g in range(8)]).astype(np.int64)


E2M1 = np.array([0.0, 0.5, 1.0, 1.5, 2.0, 3.0, 4.0, 6.0, -0.0, -0.5, -1.0, -1.5, -2.0, -3.0, -4.0, -6.0])


def pack_weight(w, fmt):
    k, n = w.shape
    w = f64(np.asarray(w, np.float32).astype(ml_dtypes.bfloat16)).reshape(k // 32, 32, n)
    amax = np.abs(w).max(1)
    if fmt == "e4m3":
        byte = np.frexp(amax)[1] - 1 + 127 - 7
    else:
        mant, ex = np.frexp(amax / 6.0)
        byte = np.where(mant > 0.5, ex, ex - 1) + 127
    byte = np.clip(np.where(amax > 0, byte, 1), 1, 254)
    scaled = (w * np.exp2(127.0 - byte)[:, None, :]).reshape(k, n).astype(np.float32)
    by_word = np.ascontiguousarray(scaled.reshape(k // 512, 128, 4, n).transpose(0, 1, 3, 2))
    if fmt == "e4m3":
        words = by_word.astype(ml_dtypes.float8_e4m3fn).view(np.uint8)
    else:
        c = by_word.astype(ml_dtypes.float4_e2m1fn).view(np.uint8) & 0xF
        words = (c[..., 0::2] | (c[..., 1::2] << 4)).reshape(k // 512, 128, 2 * n)
    return np.ascontiguousarray(words), np.ascontiguousarray(byte.astype(np.uint8).reshape(k // 512, 16, n))


def unpack_weight(words, scales, fmt):
    g, _, n = scales.shape
    words = np.ascontiguousarray(words).reshape(g, 128, n, -1)
    if fmt == "e4m3":
        vals = words.view(ml_dtypes.float8_e4m3fn).astype(np.float64)
    else:
        nib = np.empty((g, 128, n, 4), np.uint8)
        nib[..., 0::2] = words & 0xF
        nib[..., 1::2] = words >> 4
        vals = E2M1[nib]
    vals = vals * np.repeat(np.exp2(scales.astype(np.float64) - 127.0), 8, axis=1)[..., None]
    return vals.transpose(0, 1, 3, 2).reshape(g * 512, n)


K, L, M, T, S = 1536, 512, 128, 1024, 512


def setup_inputs():
    n = np.random.standard_normal
    s1 = mx_kscale(K)[:, None]
    s2 = mx_kscale(L)[:, None]
    p_w4 = pack_weight(n((K, M)) / np.sqrt(K) / s1, "e2m1")
    return {
        "xT": (n((K, T)) * s1).astype(np.float32),
        "w4_words": p_w4[0],
        "w4_scales": p_w4[1],
        "c": (n((L, S)) * s2).astype(np.float32),
        "u": (n((L, M)) / np.sqrt(L) / s2).astype(np.float32),
        "wgt": np.repeat(np.random.uniform(0.5, 2.0, (8, S)), 16, axis=0).astype(np.float32),
        "r": (n((512, 128))).astype(np.float32),
        "offs": striped8(np.stack([np.random.permutation(T)[:S] for _ in range(8)])),
    }


def reference(xT, w4_words, w4_scales, c, u, wgt, r, offs):
    idx = unstriped8(offs)
    group = np.arange(K) % 512 // 64
    xg = f64(wgt)[np.arange(K) // 4 % 128] * f64(xT)[np.arange(K)[:, None], idx[group]]
    xT_ = mxq(xg, 0, "e4m3")
    w4_ = unpack_weight(w4_words, w4_scales, "e2m1")
    c_ = mxq(f64(c), 0, "e4m3")
    u_ = mxq(f64(u), 0, "e4m3")
    y = xT_.T @ w4_ + c_.T @ u_
    return f64(r) + y

@@ -1,0 +1,172 @@
+from contextlib import ExitStack
+
+import concourse.mybir as mybir
+
+FLOPS = 2 * 512 * 128 * 2048
+
+F32 = mybir.dt.float32
+BF16 = mybir.dt.bfloat16
+I32 = mybir.dt.int32
+U32 = mybir.dt.uint32
+U16 = mybir.dt.uint16
+U8 = mybir.dt.uint8
+E4M3X4 = mybir.dt.float8_e4m3fn_x4
+E2M1X4 = mybir.dt.float4_e2m1fn_x4
+MULT = mybir.AluOpType.mult
+ADD = mybir.AluOpType.add
+
+P = 128
+PACK = 4
+T = 1024
+S = 512
+N = 128
+PASSES = 3
+HALF = 256
+
+
+def tile_list_hmix_tm_res_kernel(tc, xT, w4_words, w4_scales, c, u, wgt, r, offs, out):
+    nc = tc.nc
+    with ExitStack() as ctx:
+        held = ctx.enter_context(tc.tile_pool(name="held", bufs=1))
+        work = ctx.enter_context(tc.tile_pool(name="work", bufs=3))
+        psum = ctx.enter_context(tc.psum_pool(name="psum", bufs=1))
+
+        offsets = held.tile([P, S // 16], U16, name="offsets")
+        nc.sync.dma_start(offsets[:], offs)
+        wgt_half = [held.tile([P, HALF], F32, name=f"wgt{s}") for s in range(2)]
+        nc.scalar.dma_start(wgt_half[0][:], wgt[:, 0:HALF])
+
+        w4_sc = held.tile([P, PASSES, N], U8, name="w4_sc", align_bytes=64)
+        nc.gpsimd.memset(w4_sc[:].rearrange("p a n -> p (a n)").bitcast(I32), 0)
+
+        x_rows = xT.rearrange("(a p i) t -> a i p t", a=PASSES, i=PACK)
+        planes = {}
+
+        def load_plane(a, i):
+            planes[a, i] = held.tile([P, T], F32, name=f"plane{a}{i}")
+            nc.sync.dma_start(planes[a, i][:], x_rows[a, i])
+
+        load_plane(0, 0)
+        nc.sync.dma_start(wgt_half[1][:], wgt[:, HALF:S])
+        for i in range(1, PACK):
+            load_plane(0, i)
+        for i in range(PACK):
+            load_plane(1, i)
+        u_raw = held.tile([P, PACK, N], F32, name="u_raw")
+        nc.sync.dma_start(u_raw[:], u.rearrange("(p i) n -> p i n", i=PACK))
+        c_raw = [held.tile([P, PACK, HALF], F32, name=f"c_raw{s}") for s in range(2)]
+        c_rows = c.rearrange("(p i) j -> p i j", i=PACK)
+        load_plane(2, 0)
+        nc.sync.dma_start(c_raw[0][:], c_rows[:, :, 0:HALF])
+        load_plane(2, 1)
+        nc.sync.dma_start(c_raw[1][:], c_rows[:, :, HALF:S])
+        load_plane(2, 2)
+        load_plane(2, 3)
+        w4 = held.tile([P, PASSES, 2 * N], U8, name="w4", align_bytes=64)
+        nc.sync.dma_start(w4[:].bitcast(I32), w4_words.rearrange("a p n -> p a n").bitcast(I32))
+        for q in range(4):
+            nc.sync.dma_start(
+                w4_sc[32 * q : 32 * q + 4, :, :].bitcast(I32),
+                w4_scales[:, 4 * q : 4 * q + 4, :].rearrange("a r n -> r a n").bitcast(I32),
+            )
+        r_sb = held.tile([P, 4, N], F32, name="r_sb")
+        nc.sync.dma_start(r_sb[:], r.rearrange("(m p) n -> p m n", p=P))
+
+        codes, scales = {}, {}
+        g = {(a, s): held.tile([P, PACK, HALF], F32, name=f"g{a}{s}") for a in range(PASSES) for s in range(2)}
+        xb = {(a, s): held.tile([P, HALF, PACK], BF16, name=f"xb{a}{s}", align_bytes=64) for a in range(PASSES) for s in range(2)}
+
+        def gather(a, i, s):
+            nc.vector.tensor_tensor(
+                g[a, s][:, i, :],
+                planes[a, i][:].indirect(offsets[:, s * (HALF // 16) : (s + 1) * (HALF // 16)]),
+                wgt_half[s][:],
+                MULT,
+            )
+
+        def interleave(a, s):
+            nc.scalar.copy(xb[a, s][:], g[a, s][:].rearrange("p i j -> p j i"))
+
+        def quantize(key, b, width):
+            codes[key] = held.tile([P, width], U32, name=f"codes_{key}", align_bytes=64)
+            scales[key] = held.tile([P, width], U8, name=f"scales_{key}", align_bytes=64)
+            nc.vector.quantize_mx(
+                out=codes[key][:].bitcast(E4M3X4), scales=scales[key][:], in_=b.rearrange("p j i -> p (j i)")
+            )
+
+        acc = [psum.tile([P, N], F32, name=f"acc{m}") for m in range(4)]
+
+        def mm(m, key, col, rhs, rhs_scale, start, stop):
+            cols = slice(col, col + P)
+            nc.tensor.matmul_mx(
+                out=acc[m][:],
+                lhsT=codes[key][:, cols].bitcast(E4M3X4),
+                lhsT_scale=scales[key][:, cols],
+                rhs=rhs,
+                rhs_scale=rhs_scale,
+                start=start,
+                stop=stop,
+            )
+
+        def x_pass(a, s):
+            for h in range(2):
+                mm(2 * s + h, f"x{a}{s}", h * P, w4[:, a, :].bitcast(E2M1X4), w4_sc[:, a, :], a == 0, a == 2)
+
+        def quantize_x(a, s):
+            quantize(f"x{a}{s}", xb[a, s][:], HALF)
+            x_pass(a, s)
+
+        out_rows = out.rearrange("(m p) n -> m p n", p=P)
+
+        def finish(m):
+            y = held.tile([P, N], F32, name=f"y{m}")
+            nc.vector.tensor_tensor(y[:], acc[m][:], r_sb[:, m, :], ADD)
+            nc.sync.dma_start(out_rows[m], y[:])
+
+        ub = held.tile([P, N, PACK], BF16, name="ub", align_bytes=64)
+        cb = held.tile([P, S, PACK], BF16, name="cb", align_bytes=64)
+
+        for i, s in ((0, 0), (0, 1), (1, 0), (1, 1), (2, 0), (3, 0)):
+            gather(0, i, s)
+        interleave(0, 0)
+        gather(0, 2, 1)
+        gather(0, 3, 1)
+        interleave(0, 1)
+        gather(1, 0, 0)
+        gather(1, 0, 1)
+        gather(1, 1, 0)
+        quantize_x(0, 0)
+        gather(1, 1, 1)
+        gather(1, 2, 0)
+        quantize_x(0, 1)
+        nc.scalar.copy(ub[:], u_raw[:].rearrange("p i n -> p n i"))
+        gather(1, 3, 0)
+        interleave(1, 0)
+        gather(1, 2, 1)
+        gather(1, 3, 1)
+        interleave(1, 1)
+        for s in range(2):
+            nc.scalar.copy(cb[:, s * HALF : (s + 1) * HALF, :], c_raw[s][:].rearrange("p i j -> p j i"))
+        gather(2, 0, 0)
+        quantize("u", ub[:], N)
+        gather(2, 0, 1)
+        gather(2, 1, 0)
+        quantize_x(1, 0)
+        gather(2, 1, 1)
+        gather(2, 2, 0)
+        quantize_x(1, 1)
+        gather(2, 3, 0)
+        interleave(2, 0)
+        gather(2, 2, 1)
+        gather(2, 3, 1)
+        nc.scalar.copy(xb[2, 1][:, 0:P, :], g[2, 1][:, :, 0:P].rearrange("p i j -> p j i"))
+        quantize("c", cb[:], S)
+        for m in range(4):
+            mm(m, "c", m * P, codes["u"][:].bitcast(E4M3X4), scales["u"][:], False, False)
+        nc.vector.tensor_copy(xb[2, 1][:, P:HALF, :], g[2, 1][:, :, P:HALF].rearrange("p i j -> p j i"))
+        quantize_x(2, 0)
+        for h in range(2):
+            quantize(f"x21{h}", xb[2, 1][:, h * P : (h + 1) * P, :], P)
+            mm(2 + h, f"x21{h}", 0, w4[:, 2, :].bitcast(E2M1X4), w4_sc[:, 2, :], False, True)
+        for m in range(4):
+            finish(m)

@@ -52,16 +52,14 @@ def tile_list_hmix_tm_res_kernel(tc, xT, w4_words, w4_scales, c, u, wgt, r, offs
             load_plane(0, i)
         for i in range(PACK):
             load_plane(1, i)
-        u_raw = held.tile([P, PACK, N], F32, name="u_raw")
-        nc.sync.dma_start(u_raw[:], u.rearrange("(p i) n -> p i n", i=PACK))
-        c_raw = [held.tile([P, PACK, HALF], F32, name=f"c_raw{s}") for s in range(2)]
-        c_rows = c.rearrange("(p i) j -> p i j", i=PACK)
         load_plane(2, 0)
-        nc.sync.dma_start(c_raw[0][:], c_rows[:, :, 0:HALF])
         load_plane(2, 1)
-        nc.sync.dma_start(c_raw[1][:], c_rows[:, :, HALF:S])
+        c_raw = held.tile([P, PACK, S], F32, name="c_raw")
+        nc.sync.dma_start(c_raw[:], c.rearrange("(p i) j -> p i j", i=PACK))
         load_plane(2, 2)
         load_plane(2, 3)
+        u_raw = held.tile([P, PACK, N], F32, name="u_raw")
+        nc.sync.dma_start(u_raw[:], u.rearrange("(p i) n -> p i n", i=PACK))
         w4 = held.tile([P, PASSES, 2 * N], U8, name="w4", align_bytes=64)
         nc.sync.dma_start(w4[:].bitcast(I32), w4_words.rearrange("a p n -> p a n").bitcast(I32))
         for q in range(4):
@@ -126,11 +124,10 @@ def tile_list_hmix_tm_res_kernel(tc, xT, w4_words, w4_scales, c, u, wgt, r, offs
         ub = held.tile([P, N, PACK], BF16, name="ub", align_bytes=64)
         cb = held.tile([P, S, PACK], BF16, name="cb", align_bytes=64)
 
-        for i, s in ((0, 0), (0, 1), (1, 0), (1, 1), (2, 0), (3, 0)):
-            gather(0, i, s)
+        for i in range(PACK):
+            gather(0, i, 0)
+            gather(0, i, 1)
         interleave(0, 0)
-        gather(0, 2, 1)
-        gather(0, 3, 1)
         interleave(0, 1)
         gather(1, 0, 0)
         gather(1, 0, 1)
@@ -139,16 +136,16 @@ def tile_list_hmix_tm_res_kernel(tc, xT, w4_words, w4_scales, c, u, wgt, r, offs
         gather(1, 1, 1)
         gather(1, 2, 0)
         quantize_x(0, 1)
-        nc.scalar.copy(ub[:], u_raw[:].rearrange("p i n -> p n i"))
         gather(1, 3, 0)
         interleave(1, 0)
         gather(1, 2, 1)
         gather(1, 3, 1)
         interleave(1, 1)
         for s in range(2):
-            nc.scalar.copy(cb[:, s * HALF : (s + 1) * HALF, :], c_raw[s][:].rearrange("p i j -> p j i"))
+            cols = slice(s * HALF, (s + 1) * HALF)
+            nc.scalar.copy(cb[:, cols, :], c_raw[:, :, cols].rearrange("p i j -> p j i"))
+        nc.scalar.copy(ub[:], u_raw[:].rearrange("p i n -> p n i"))
         gather(2, 0, 0)
-        quantize("u", ub[:], N)
         gather(2, 0, 1)
         gather(2, 1, 0)
         quantize_x(1, 0)
@@ -161,12 +158,14 @@ def tile_list_hmix_tm_res_kernel(tc, xT, w4_words, w4_scales, c, u, wgt, r, offs
         gather(2, 3, 1)
         nc.scalar.copy(xb[2, 1][:, 0:P, :], g[2, 1][:, :, 0:P].rearrange("p i j -> p j i"))
         quantize("c", cb[:], S)
+        quantize("u", ub[:], N)
         for m in range(4):
             mm(m, "c", m * P, codes["u"][:].bitcast(E4M3X4), scales["u"][:], False, False)
-        nc.vector.tensor_copy(xb[2, 1][:, P:HALF, :], g[2, 1][:, :, P:HALF].rearrange("p i j -> p j i"))
         quantize_x(2, 0)
+        nc.vector.tensor_copy(xb[2, 1][:, P:HALF, :], g[2, 1][:, :, P:HALF].rearrange("p i j -> p j i"))
+        finish(0)
         for h in range(2):
             quantize(f"x21{h}", xb[2, 1][:, h * P : (h + 1) * P, :], P)
             mm(2 + h, f"x21{h}", 0, w4[:, 2, :].bitcast(E2M1X4), w4_sc[:, 2, :], False, True)
-        for m in range(4):
+        for m in range(1, 4):
             finish(m)

@@ -34,7 +34,7 @@ def tile_list_hmix_tm_res_kernel(tc, xT, w4_words, w4_scales, c, u, wgt, r, offs
         offsets = held.tile([P, S // 16], U16, name="offsets")
         nc.sync.dma_start(offsets[:], offs)
         wgt_half = [held.tile([P, HALF], F32, name=f"wgt{s}") for s in range(2)]
-        nc.scalar.dma_start(wgt_half[0][:], wgt[:, 0:HALF])
+        nc.sync.dma_start(wgt_half[0][:], wgt[:, 0:HALF])
 
         w4_sc = held.tile([P, PASSES, N], U8, name="w4_sc", align_bytes=64)
         nc.gpsimd.memset(w4_sc[:].rearrange("p a n -> p (a n)").bitcast(I32), 0)
@@ -72,7 +72,7 @@ def tile_list_hmix_tm_res_kernel(tc, xT, w4_words, w4_scales, c, u, wgt, r, offs
 
         codes, scales = {}, {}
         g = {(a, s): held.tile([P, PACK, HALF], F32, name=f"g{a}{s}") for a in range(PASSES) for s in range(2)}
-        xb = {(a, s): held.tile([P, HALF, PACK], BF16, name=f"xb{a}{s}", align_bytes=64) for a in range(PASSES) for s in range(2)}
+        xb = [held.tile([P, S, PACK], BF16, name=f"xb{a}", align_bytes=64) for a in range(PASSES)]
 
         def gather(a, i, s):
             nc.vector.tensor_tensor(
@@ -82,8 +82,10 @@ def tile_list_hmix_tm_res_kernel(tc, xT, w4_words, w4_scales, c, u, wgt, r, offs
                 MULT,
             )
 
-        def interleave(a, s):
-            nc.scalar.copy(xb[a, s][:], g[a, s][:].rearrange("p i j -> p j i"))
+        def interleave(a, s, lo=0, hi=HALF, copy=nc.scalar.copy):
+            copy(
+                xb[a][:, s * HALF + lo : s * HALF + hi, :], g[a, s][:, :, lo:hi].rearrange("p i j -> p j i")
+            )
 
         def quantize(key, b, width):
             codes[key] = held.tile([P, width], U32, name=f"codes_{key}", align_bytes=64)
@@ -106,13 +108,11 @@ def tile_list_hmix_tm_res_kernel(tc, xT, w4_words, w4_scales, c, u, wgt, r, offs
                 stop=stop,
             )
 
-        def x_pass(a, s):
-            for h in range(2):
-                mm(2 * s + h, f"x{a}{s}", h * P, w4[:, a, :].bitcast(E2M1X4), w4_sc[:, a, :], a == 0, a == 2)
-
-        def quantize_x(a, s):
-            quantize(f"x{a}{s}", xb[a, s][:], HALF)
-            x_pass(a, s)
+        def quantize_x(a, lo, hi):
+            key = f"x{a}{lo}"
+            quantize(key, xb[a][:, lo:hi, :], hi - lo)
+            for m in range(lo // P, hi // P):
+                mm(m, key, m * P - lo, w4[:, a, :].bitcast(E2M1X4), w4_sc[:, a, :], a == 0, a == PASSES - 1)
 
         out_rows = out.rearrange("(m p) n -> m p n", p=P)
 
@@ -129,13 +129,11 @@ def tile_list_hmix_tm_res_kernel(tc, xT, w4_words, w4_scales, c, u, wgt, r, offs
             gather(0, i, 1)
         interleave(0, 0)
         interleave(0, 1)
-        gather(1, 0, 0)
-        gather(1, 0, 1)
-        gather(1, 1, 0)
-        quantize_x(0, 0)
-        gather(1, 1, 1)
+        for i in range(2):
+            gather(1, i, 0)
+            gather(1, i, 1)
+        quantize_x(0, 0, S)
         gather(1, 2, 0)
-        quantize_x(0, 1)
         gather(1, 3, 0)
         interleave(1, 0)
         gather(1, 2, 1)
@@ -145,27 +143,24 @@ def tile_list_hmix_tm_res_kernel(tc, xT, w4_words, w4_scales, c, u, wgt, r, offs
             cols = slice(s * HALF, (s + 1) * HALF)
             nc.scalar.copy(cb[:, cols, :], c_raw[:, :, cols].rearrange("p i j -> p j i"))
         nc.scalar.copy(ub[:], u_raw[:].rearrange("p i n -> p n i"))
-        gather(2, 0, 0)
-        gather(2, 0, 1)
-        gather(2, 1, 0)
-        quantize_x(1, 0)
-        gather(2, 1, 1)
+        for i in range(2):
+            gather(2, i, 0)
+            gather(2, i, 1)
+        quantize_x(1, 0, S)
         gather(2, 2, 0)
-        quantize_x(1, 1)
         gather(2, 3, 0)
         interleave(2, 0)
         gather(2, 2, 1)
         gather(2, 3, 1)
-        nc.scalar.copy(xb[2, 1][:, 0:P, :], g[2, 1][:, :, 0:P].rearrange("p i j -> p j i"))
+        interleave(2, 1, 0, P)
         quantize("c", cb[:], S)
         quantize("u", ub[:], N)
         for m in range(4):
             mm(m, "c", m * P, codes["u"][:].bitcast(E4M3X4), scales["u"][:], False, False)
-        quantize_x(2, 0)
-        nc.vector.tensor_copy(xb[2, 1][:, P:HALF, :], g[2, 1][:, :, P:HALF].rearrange("p i j -> p j i"))
+        quantize_x(2, 0, HALF)
+        interleave(2, 1, P, HALF, nc.vector.tensor_copy)
+        quantize_x(2, HALF, HALF + P)
         finish(0)
-        for h in range(2):
-            quantize(f"x21{h}", xb[2, 1][:, h * P : (h + 1) * P, :], P)
-            mm(2 + h, f"x21{h}", 0, w4[:, 2, :].bitcast(E2M1X4), w4_sc[:, 2, :], False, True)
+        quantize_x(2, HALF + P, S)
         for m in range(1, 4):
             finish(m)

@@ -82,10 +82,14 @@ def tile_list_hmix_tm_res_kernel(tc, xT, w4_words, w4_scales, c, u, wgt, r, offs
                 MULT,
             )
 
-        def interleave(a, s, lo=0, hi=HALF, copy=nc.scalar.copy):
+        def blocked_copy(copy, dst, rows):
             copy(
-                xb[a][:, s * HALF + lo : s * HALF + hi, :], g[a, s][:, :, lo:hi].rearrange("p i j -> p j i")
+                dst.rearrange("p (b k) i -> p b i k", k=4),
+                rows.rearrange("p i (b k) -> p b i k", k=4),
             )
+
+        def interleave(a, s, lo=0, hi=HALF, copy=nc.scalar.copy):
+            blocked_copy(copy, xb[a][:, s * HALF + lo : s * HALF + hi, :], g[a, s][:, :, lo:hi])
 
         def quantize(key, b, width):
             codes[key] = held.tile([P, width], U32, name=f"codes_{key}", align_bytes=64)
@@ -141,8 +145,8 @@ def tile_list_hmix_tm_res_kernel(tc, xT, w4_words, w4_scales, c, u, wgt, r, offs
         interleave(1, 1)
         for s in range(2):
             cols = slice(s * HALF, (s + 1) * HALF)
-            nc.scalar.copy(cb[:, cols, :], c_raw[:, :, cols].rearrange("p i j -> p j i"))
-        nc.scalar.copy(ub[:], u_raw[:].rearrange("p i n -> p n i"))
+            blocked_copy(nc.scalar.copy, cb[:, cols, :], c_raw[:, :, cols])
+        blocked_copy(nc.scalar.copy, ub[:], u_raw[:])
         for i in range(2):
             gather(2, i, 0)
             gather(2, i, 1)

from contextlib import ExitStack

import concourse.mybir as mybir

FLOPS = 2 * 512 * 128 * 2048

F32 = mybir.dt.float32
BF16 = mybir.dt.bfloat16
I32 = mybir.dt.int32
U32 = mybir.dt.uint32
U16 = mybir.dt.uint16
U8 = mybir.dt.uint8
E4M3X4 = mybir.dt.float8_e4m3fn_x4
E2M1X4 = mybir.dt.float4_e2m1fn_x4
MULT = mybir.AluOpType.mult
ADD = mybir.AluOpType.add

P = 128
PACK = 4
T = 1024
S = 512
N = 128
PASSES = 3
HALF = 256


def tile_list_hmix_tm_res_kernel(tc, xT, w4_words, w4_scales, c, u, wgt, r, offs, out):
    nc = tc.nc
    with ExitStack() as ctx:
        held = ctx.enter_context(tc.tile_pool(name="held", bufs=1))
        work = ctx.enter_context(tc.tile_pool(name="work", bufs=3))
        psum = ctx.enter_context(tc.psum_pool(name="psum", bufs=1))

        offsets = held.tile([P, S // 16], U16, name="offsets")
        nc.sync.dma_start(offsets[:], offs)
        wgt_half = [held.tile([P, HALF], F32, name=f"wgt{s}") for s in range(2)]
        nc.sync.dma_start(wgt_half[0][:], wgt[:, 0:HALF])

        w4_sc = held.tile([P, PASSES, N], U8, name="w4_sc", align_bytes=64)
        nc.gpsimd.memset(w4_sc[:].rearrange("p a n -> p (a n)").bitcast(I32), 0)

        x_rows = xT.rearrange("(a p i) t -> a i p t", a=PASSES, i=PACK)
        planes = {}

        def load_plane(a, i):
            planes[a, i] = held.tile([P, T], F32, name=f"plane{a}{i}")
            nc.sync.dma_start(planes[a, i][:], x_rows[a, i])

        load_plane(0, 0)
        nc.sync.dma_start(wgt_half[1][:], wgt[:, HALF:S])
        for i in range(1, PACK):
            load_plane(0, i)
        for i in range(PACK):
            load_plane(1, i)
        load_plane(2, 0)
        load_plane(2, 1)
        c_raw = held.tile([P, PACK, S], F32, name="c_raw")
        nc.sync.dma_start(c_raw[:], c.rearrange("(p i) j -> p i j", i=PACK))
        load_plane(2, 2)
        load_plane(2, 3)
        u_raw = held.tile([P, PACK, N], F32, name="u_raw")
        nc.sync.dma_start(u_raw[:], u.rearrange("(p i) n -> p i n", i=PACK))
        w4 = held.tile([P, PASSES, 2 * N], U8, name="w4", align_bytes=64)
        nc.sync.dma_start(w4[:].bitcast(I32), w4_words.rearrange("a p n -> p a n").bitcast(I32))
        for q in range(4):
            nc.sync.dma_start(
                w4_sc[32 * q : 32 * q + 4, :, :].bitcast(I32),
                w4_scales[:, 4 * q : 4 * q + 4, :].rearrange("a r n -> r a n").bitcast(I32),
            )
        r_sb = held.tile([P, 4, N], F32, name="r_sb")
        nc.sync.dma_start(r_sb[:], r.rearrange("(m p) n -> p m n", p=P))

        codes, scales = {}, {}
        g = {(a, s): held.tile([P, PACK, HALF], F32, name=f"g{a}{s}") for a in range(PASSES) for s in range(2)}
        xb = [held.tile([P, S, PACK], BF16, name=f"xb{a}", align_bytes=64) for a in range(PASSES)]

        def gather(a, i, s):
            nc.vector.tensor_tensor(
                g[a, s][:, i, :],
                planes[a, i][:].indirect(offsets[:, s * (HALF // 16) : (s + 1) * (HALF // 16)]),
                wgt_half[s][:],
                MULT,
            )

        def blocked_copy(copy, dst, rows):
            copy(
                dst.rearrange("p (b k) i -> p b i k", k=4),
                rows.rearrange("p i (b k) -> p b i k", k=4),
            )

        def interleave(a, s, lo=0, hi=HALF, copy=nc.scalar.copy):
            blocked_copy(copy, xb[a][:, s * HALF + lo : s * HALF + hi, :], g[a, s][:, :, lo:hi])

        def quantize(key, b, width):
            codes[key] = held.tile([P, width], U32, name=f"codes_{key}", align_bytes=64)
            scales[key] = held.tile([P, width], U8, name=f"scales_{key}", align_bytes=64)
            nc.vector.quantize_mx(
                out=codes[key][:].bitcast(E4M3X4), scales=scales[key][:], in_=b.rearrange("p j i -> p (j i)")
            )

        acc = [psum.tile([P, N], F32, name=f"acc{m}") for m in range(4)]

        def mm(m, key, col, rhs, rhs_scale, start, stop):
            cols = slice(col, col + P)
            nc.tensor.matmul_mx(
                out=acc[m][:],
                lhsT=codes[key][:, cols].bitcast(E4M3X4),
                lhsT_scale=scales[key][:, cols],
                rhs=rhs,
                rhs_scale=rhs_scale,
                start=start,
                stop=stop,
            )

        def quantize_x(a, lo, hi):
            key = f"x{a}{lo}"
            quantize(key, xb[a][:, lo:hi, :], hi - lo)
            for m in range(lo // P, hi // P):
                mm(m, key, m * P - lo, w4[:, a, :].bitcast(E2M1X4), w4_sc[:, a, :], a == 0, a == PASSES - 1)

        out_rows = out.rearrange("(m p) n -> m p n", p=P)

        def finish(m):
            y = held.tile([P, N], F32, name=f"y{m}")
            nc.vector.tensor_tensor(y[:], acc[m][:], r_sb[:, m, :], ADD)
            nc.sync.dma_start(out_rows[m], y[:])

        ub = held.tile([P, N, PACK], BF16, name="ub", align_bytes=64)
        cb = held.tile([P, S, PACK], BF16, name="cb", align_bytes=64)

        for i in range(PACK):
            gather(0, i, 0)
            gather(0, i, 1)
        interleave(0, 0)
        interleave(0, 1)
        for i in range(2):
            gather(1, i, 0)
            gather(1, i, 1)
        quantize_x(0, 0, S)
        gather(1, 2, 0)
        gather(1, 3, 0)
        interleave(1, 0)
        gather(1, 2, 1)
        gather(1, 3, 1)
        interleave(1, 1)
        for s in range(2):
            cols = slice(s * HALF, (s + 1) * HALF)
            blocked_copy(nc.scalar.copy, cb[:, cols, :], c_raw[:, :, cols])
        blocked_copy(nc.scalar.copy, ub[:], u_raw[:])
        for i in range(2):
            gather(2, i, 0)
            gather(2, i, 1)
        quantize_x(1, 0, S)
        gather(2, 2, 0)
        gather(2, 3, 0)
        interleave(2, 0)
        gather(2, 2, 1)
        gather(2, 3, 1)
        interleave(2, 1, 0, P)
        quantize("c", cb[:], S)
        quantize("u", ub[:], N)
        for m in range(4):
            mm(m, "c", m * P, codes["u"][:].bitcast(E4M3X4), scales["u"][:], False, False)
        quantize_x(2, 0, HALF)
        interleave(2, 1, P, HALF, nc.vector.tensor_copy)
        quantize_x(2, HALF, HALF + P)
        finish(0)
        quantize_x(2, HALF + P, S)
        for m in range(1, 4):
            finish(m)
